import numpy as np
import ml_dtypes


def mxq(x, axis, fmt="e4m3"):
    dtype, down = {"e4m3": (ml_dtypes.float8_e4m3fn, 7), "e5m2": (ml_dtypes.float8_e5m2, 14)}[fmt]
    v = np.moveaxis(np.asarray(x, np.float32).astype(ml_dtypes.bfloat16).astype(np.float64), axis, -1)
    blocks = v.reshape(v.shape[:-1] + (-1, 32))
    amax = np.abs(blocks).max(-1, keepdims=True)
    byte = np.maximum(np.where(amax > 0, np.frexp(amax)[1] - 1 + 127, 0) - down, 1)
    scale = np.exp2(byte - 127.0)
    codes = (blocks / scale).astype(np.float32).astype(dtype).astype(np.float64)
    return np.moveaxis((codes * scale).reshape(v.shape), -1, axis)


WIDE = False


def mx_kscale(k):
    if not WIDE:
        return np.ones(k)
    levels = np.array([10, -10, 5, -5, 0])
    if k % 512:
        return np.exp2(np.random.permutation(np.resize(levels, k // 32))).repeat(32)
    a = np.empty((k // 512, 16))
    for p in range(k // 512):
        a[p, :8] = np.random.permutation(np.resize(levels, 8))
        for g in range(8):
            far = levels[np.abs(levels - a[p, g]) >= 10]
            a[p, g + 8] = far[np.random.randint(len(far))]
    return np.exp2(a.ravel()).repeat(32)


def f64(x):
    return np.asarray(x).astype(np.float64)


def striped(idx):
    return np.tile(idx.reshape(-1, 16).T, (8, 1)).astype(np.uint16)


def unstriped(offs):
    return offs[:16].T.reshape(-1).astype(np.int64)


def striped8(idx):
    return np.concatenate([x.reshape(-1, 16).T for x in idx]).astype(np.uint16)


def runs(offs, k):
    lists = np.stack([offs[16 * r : 16 * r + 16].T.reshape(-1) for r in range(8)]).astype(np.int64)
    return lists[np.arange(k) % 512 // 64]


def pack_weight(w):
    k, n = w.shape
    w = f64(np.asarray(w, np.float32).astype(ml_dtypes.bfloat16)).reshape(k // 32, 32, n)
    amax = np.abs(w).max(1)
    byte = np.clip(np.where(amax > 0, np.frexp(amax)[1] - 1 + 127 - 7, 1), 1, 254)
    scaled = (w * np.exp2(127.0 - byte)[:, None, :]).reshape(k, n).astype(np.float32)
    words = np.ascontiguousarray(scaled.reshape(k // 512, 128, 4, n).transpose(0, 1, 3, 2)).astype(ml_dtypes.float8_e4m3fn).view(np.uint8)
    return words, np.ascontiguousarray(byte.astype(np.uint8).reshape(k // 512, 16, n))


def unpack_weight(words, scales):
    g, p, n, _ = words.shape
    vals = np.ascontiguousarray(words).view(ml_dtypes.float8_e4m3fn).astype(np.float64) * np.repeat(np.exp2(scales.astype(np.float64) - 127.0), 8, axis=1)[..., None]
    return vals.transpose(0, 1, 3, 2).reshape(g * 512, n)


def relu(v):
    return np.maximum(v, 0.0)


K, T, S, N, G, H = 512, 2048, 512, 512, 2048, 512


def setup_inputs():
    n = np.random.standard_normal
    s = mx_kscale(K)[:, None]
    u = mx_kscale(H)
    packed_xT = pack_weight(n((K, T)) * s)
    packed_dT = pack_weight(n((K, G)) / s)
    return {
        "x_words": packed_xT[0],
        "x_scales": packed_xT[1],
        "d_words": packed_dT[0],
        "d_scales": packed_dT[1],
        "gn": (np.random.uniform(0.5, 1.5, (H, 1)) * u[:, None]).astype(np.float32),
        "w1": (n((H, N)) / np.sqrt(H) / u[:, None]).astype(np.float32),
        "offs": striped(np.random.permutation(T)[:S]),
        "k1": striped8(np.random.randint(0, G, (8, H))),
        "k2": striped8(np.random.randint(0, G, (8, H))),
    }


def reference(x_words, x_scales, d_words, d_scales, gn, w1, offs, k1, k2):
    d_k2 = unpack_weight(d_words, d_scales)[np.arange(K)[:, None], runs(k2, K)]
    xq = unpack_weight(x_words, x_scales)[:, unstriped(offs)]
    d_k1 = unpack_weight(d_words, d_scales)[np.arange(K)[:, None], runs(k1, K)]
    h = relu(0.0625 * (d_k1.T @ xq))
    z = f64(gn) * h
    hw = mxq(f64(w1), 0, "e4m3").T @ mxq(z, 0, "e4m3")
    return 0.0625 * (d_k2.T @ xq) + hw

@@ -1,0 +1,176 @@
+from contextlib import ExitStack
+
+import concourse.mybir as mybir
+
+F32 = mybir.dt.float32
+BF16 = mybir.dt.bfloat16
+I32 = mybir.dt.int32
+U32 = mybir.dt.uint32
+U16 = mybir.dt.uint16
+U8 = mybir.dt.uint8
+FP8X4 = mybir.dt.float8_e4m3fn_x4
+ALU = mybir.AluOpType
+ACT = mybir.ActivationFunctionType
+
+P = 128
+PACK = 4
+K, T, S, N, G, H = 512, 2048, 512, 512, 2048, 512
+CHUNK = 128
+HALF = 256
+FLOPS = 2 * K * H * S + 2 * K * N * S + 2 * H * N * S
+
+
+def tile_picked_pqskip_relu_p_kernel(
+    tc, x_words, x_scales, d_words, d_scales, gn, w1, offs, k1, k2, out
+):
+    nc = tc.nc
+    with ExitStack() as ctx:
+        keep = ctx.enter_context(tc.tile_pool(name="keep", bufs=1))
+        psum = ctx.enter_context(tc.psum_pool(name="psum", bufs=1))
+
+        k1_list = keep.tile([P, H // 16], U16, name="k1_list")
+        k2_list = keep.tile([P, N // 16], U16, name="k2_list")
+        offs_list = keep.tile([P, S // 16], U16, name="offs_list")
+        d_bytes = keep.tile([P, G], U8, name="d_bytes", tag="reuse0", align_bytes=64)
+        x_bytes = keep.tile([P, T], U8, name="x_bytes", tag="reuse1", align_bytes=64)
+        d_table = keep.tile([P, G], I32, name="d_table", align_bytes=64)
+        x_table = keep.tile([P, T], I32, name="x_table", align_bytes=64)
+        gain = keep.tile([P, PACK], F32, name="gain")
+        planes = keep.tile([P, H + N + S], U8, name="planes", align_bytes=64)
+
+        nc.vector.memset(d_bytes[:].bitcast(I32), 0)
+        nc.gpsimd.memset(x_bytes[:].bitcast(I32), 0)
+        nc.gpsimd.memset(planes[:].bitcast(I32), 0)
+        nc.sync.dma_start(k1_list[:], k1)
+        nc.sync.dma_start(k2_list[:], k2)
+        nc.sync.dma_start(offs_list[:], offs)
+        for table, scales in ((d_bytes, d_scales), (x_bytes, x_scales)):
+            rows = scales[0].rearrange("(g e) c -> e g c", e=2)
+            for e in range(2):
+                nc.scalar.dma_start(table[e:P:16, :].bitcast(I32), rows[e].bitcast(I32))
+        nc.sync.dma_start(d_table[:], d_words[0].rearrange("p c r -> p (c r)").bitcast(I32))
+        nc.sync.dma_start(x_table[:], x_words[0].rearrange("p c r -> p (c r)").bitcast(I32))
+        nc.gpsimd.dma_start(gain[:], gn.rearrange("(p t) o -> p (t o)", t=PACK))
+
+        picked_bytes = keep.tile([P, H + N + S], U8, name="picked_bytes", align_bytes=64)
+        k1_cols, k2_cols, x_cols = slice(0, H), slice(H, H + N), slice(H + N, H + N + S)
+        nc.vector.tensor_copy(picked_bytes[:, k1_cols], d_bytes[:].indirect(k1_list[:]))
+        nc.vector.tensor_copy(picked_bytes[:, k2_cols], d_bytes[:].indirect(k2_list[:]))
+        nc.vector.tensor_copy(picked_bytes[:, x_cols], x_bytes[:].indirect(offs_list[:]))
+        for c in range(4):
+            src = 16 * (c // 2) + c % 2
+            nc.scalar.dma_start(planes[c:P:32, :].bitcast(I32), picked_bytes[src:P:32, :].bitcast(I32))
+
+        w_rows = w1.rearrange("(p j) n -> p j n", j=PACK)
+        w_raw = []
+        for hf in range(2):
+            raw = keep.tile([P, PACK, HALF], F32, name=f"w_raw{hf}", tag=f"reuse{hf}", align_bytes=64)
+            nc.sync.dma_start(raw[:], w_rows[:, :, hf * HALF : (hf + 1) * HALF])
+            w_raw.append(raw)
+
+        d2_words = keep.tile([P, N], U32, name="d2_words", align_bytes=64)
+        xq_words = keep.tile([P, S], U32, name="xq_words", align_bytes=64)
+        d1_picked = keep.tile([P, H], U32, name="d1_picked", align_bytes=64)
+        nc.vector.tensor_copy(d2_words[:], d_table[:].bitcast(U32).indirect(k2_list[:]))
+        nc.vector.tensor_copy(xq_words[:], x_table[:].bitcast(U32).indirect(offs_list[:]))
+        nc.vector.tensor_copy(d1_picked[:], d_table[:].bitcast(U32).indirect(k1_list[:]))
+
+        def x_operand(tok):
+            return dict(rhs=xq_words[:, tok].bitcast(FP8X4), rhs_scale=planes[:, H + N + tok.start : H + N + tok.stop])
+
+        def shortcut(acc, m, tok):
+            nc.tensor.matmul_mx(
+                out=acc,
+                lhsT=d2_words[:, m * P : (m + 1) * P].bitcast(FP8X4),
+                lhsT_scale=planes[:, H + m * P : H + (m + 1) * P],
+                start=True,
+                stop=False,
+                **x_operand(tok),
+            )
+
+        out_acc = [[], []]
+        for m in range(N // P):
+            acc = psum.tile([P, HALF], F32, name=f"out_acc0_{m}", tag=f"out_bank{m}")
+            shortcut(acc[:], m, slice(0, HALF))
+            out_acc[0].append(acc)
+
+        d1_words = keep.tile([P, H], I32, name="d1_words", align_bytes=64)
+        d1_scales = keep.tile([P, H], U8, name="d1_scales", align_bytes=64)
+        nc.vector.tensor_copy(
+            d1_words[:].rearrange("p (t m) -> p m t", t=PACK),
+            d1_picked[:].bitcast(I32).rearrange("p (m t) -> p m t", t=PACK),
+        )
+        nc.vector.tensor_copy(
+            d1_scales[:].rearrange("p (t m) -> p m t", t=PACK),
+            planes[:, k1_cols].rearrange("p (m t) -> p m t", t=PACK),
+        )
+
+        hidden = []
+        for ch in range(S // CHUNK):
+            acc = psum.tile([P, PACK, CHUNK], F32, name=f"hidden{ch}", tag=f"hidden_bank{ch}")
+            for t in range(PACK):
+                nc.tensor.matmul_mx(
+                    out=acc[:, t, :],
+                    lhsT=d1_words[:, t * P : (t + 1) * P].bitcast(FP8X4),
+                    lhsT_scale=d1_scales[:, t * P : (t + 1) * P],
+                    start=True,
+                    stop=True,
+                    **x_operand(slice(ch * CHUNK, (ch + 1) * CHUNK)),
+                )
+            hidden.append(acc)
+
+        w_codes, w_scales = [], []
+        for hf in range(2):
+            grouped = keep.tile([P, HALF, PACK], BF16, name=f"w_grouped{hf}", align_bytes=64)
+            nc.scalar.activation(
+                grouped[:].rearrange("p (c i) j -> p c j i", i=4),
+                w_raw[hf][:].rearrange("p j (c i) -> p c j i", i=4),
+                ACT.Copy,
+            )
+            codes = keep.tile([P, HALF], U32, name=f"w_codes{hf}", align_bytes=64)
+            scales = keep.tile([P, HALF], U8, name=f"w_scales{hf}", align_bytes=64)
+            nc.vector.quantize_mx(
+                out=codes[:].bitcast(FP8X4), scales=scales[:], in_=grouped[:].rearrange("p n j -> p (n j)")
+            )
+            w_codes.append(codes)
+            w_scales.append(scales)
+
+        gain_wide = gain[:].unsqueeze(1).to_broadcast([P, CHUNK, PACK])
+        for hf in range(2):
+            z = keep.tile([P, HALF, PACK], BF16, name=f"z{hf}", align_bytes=64)
+            for c in range(HALF // CHUNK):
+                nc.vector.scalar_tensor_tensor(
+                    out=z[:, c * CHUNK : (c + 1) * CHUNK, :],
+                    in0=hidden[2 * hf + c][:].rearrange("p t s -> p s t"),
+                    scalar=0.0,
+                    in1=gain_wide,
+                    op0=ALU.max,
+                    op1=ALU.mult,
+                )
+            z_codes = keep.tile([P, HALF], U32, name=f"z_codes{hf}", align_bytes=64)
+            z_scales = keep.tile([P, HALF], U8, name=f"z_scales{hf}", align_bytes=64)
+            nc.vector.quantize_mx(
+                out=z_codes[:].bitcast(FP8X4), scales=z_scales[:], in_=z[:].rearrange("p s t -> p (s t)")
+            )
+            if hf == 1:
+                for m in range(N // P):
+                    acc = psum.tile([P, HALF], F32, name=f"out_acc1_{m}", tag=f"hidden_bank{m}")
+                    shortcut(acc[:], m, slice(HALF, S))
+                    out_acc[1].append(acc)
+            for m in range(N // P):
+                cols = slice((m % 2) * P, (m % 2 + 1) * P)
+                nc.tensor.matmul_mx(
+                    out=out_acc[hf][m][:],
+                    lhsT=w_codes[m // 2][:, cols].bitcast(FP8X4),
+                    lhsT_scale=w_scales[m // 2][:, cols],
+                    rhs=z_codes[:].bitcast(FP8X4),
+                    rhs_scale=z_scales[:],
+                    start=False,
+                    stop=True,
+                )
+                result = keep.tile([P, HALF], F32, name=f"result{hf}_{m}")
+                if hf == 1 and m % 2 == 1:
+                    nc.vector.tensor_scalar(result[:], out_acc[hf][m][:], 0.0625, None, ALU.mult)
+                else:
+                    nc.scalar.activation(result[:], out_acc[hf][m][:], ACT.Copy, scale=0.0625)
+                nc.sync.dma_start(out[m * P : (m + 1) * P, hf * HALF : (hf + 1) * HALF], result[:])

@@ -31,26 +31,34 @@ def tile_picked_pqskip_relu_p_kernel(
         k1_list = keep.tile([P, H // 16], U16, name="k1_list")
         k2_list = keep.tile([P, N // 16], U16, name="k2_list")
         offs_list = keep.tile([P, S // 16], U16, name="offs_list")
-        d_bytes = keep.tile([P, G], U8, name="d_bytes", tag="reuse0", align_bytes=64)
-        x_bytes = keep.tile([P, T], U8, name="x_bytes", tag="reuse1", align_bytes=64)
+        d_bytes = keep.tile([P, G], U8, name="d_bytes", align_bytes=64)
+        x_bytes = keep.tile([P, T], U8, name="x_bytes", tag="x_bytes_then_w1", align_bytes=64)
         d_table = keep.tile([P, G], I32, name="d_table", align_bytes=64)
         x_table = keep.tile([P, T], I32, name="x_table", align_bytes=64)
         gain = keep.tile([P, PACK], F32, name="gain")
         planes = keep.tile([P, H + N + S], U8, name="planes", align_bytes=64)
 
-        nc.vector.memset(d_bytes[:].bitcast(I32), 0)
-        nc.gpsimd.memset(x_bytes[:].bitcast(I32), 0)
-        nc.gpsimd.memset(planes[:].bitcast(I32), 0)
+        nc.vector.memset(planes[:].bitcast(I32), 0)
+
+        def block_rows(scales):
+            return scales[0].bitcast(I32).unsqueeze(1).to_broadcast([16, 8, G // 4])
+
+        w_rows = w1.rearrange("(p j) n -> p j n", j=PACK)
+
+        def load_w1_half(hf, tag):
+            raw = keep.tile([P, PACK, HALF], F32, name=f"w_raw{hf}", tag=tag, align_bytes=64)
+            nc.sync.dma_start(raw[:], w_rows[:, :, hf * HALF : (hf + 1) * HALF])
+            return raw
+
         nc.sync.dma_start(k1_list[:], k1)
+        nc.sync.dma_start(d_bytes[:].bitcast(I32), block_rows(d_scales))
         nc.sync.dma_start(k2_list[:], k2)
+        nc.sync.dma_start(x_bytes[:].bitcast(I32), block_rows(x_scales))
         nc.sync.dma_start(offs_list[:], offs)
-        for table, scales in ((d_bytes, d_scales), (x_bytes, x_scales)):
-            rows = scales[0].rearrange("(g e) c -> e g c", e=2)
-            for e in range(2):
-                nc.scalar.dma_start(table[e:P:16, :].bitcast(I32), rows[e].bitcast(I32))
-        nc.sync.dma_start(d_table[:], d_words[0].rearrange("p c r -> p (c r)").bitcast(I32))
         nc.sync.dma_start(x_table[:], x_words[0].rearrange("p c r -> p (c r)").bitcast(I32))
-        nc.gpsimd.dma_start(gain[:], gn.rearrange("(p t) o -> p (t o)", t=PACK))
+        nc.sync.dma_start(d_table[:], d_words[0].rearrange("p c r -> p (c r)").bitcast(I32))
+        w_raw = [load_w1_half(0, "w1_first")]
+        nc.sync.dma_start(gain[:], gn.rearrange("(p t) o -> p (t o)", t=PACK))
 
         picked_bytes = keep.tile([P, H + N + S], U8, name="picked_bytes", align_bytes=64)
         k1_cols, k2_cols, x_cols = slice(0, H), slice(H, H + N), slice(H + N, H + N + S)
@@ -58,21 +66,16 @@ def tile_picked_pqskip_relu_p_kernel(
         nc.vector.tensor_copy(picked_bytes[:, k2_cols], d_bytes[:].indirect(k2_list[:]))
         nc.vector.tensor_copy(picked_bytes[:, x_cols], x_bytes[:].indirect(offs_list[:]))
         for c in range(4):
-            src = 16 * (c // 2) + c % 2
-            nc.scalar.dma_start(planes[c:P:32, :].bitcast(I32), picked_bytes[src:P:32, :].bitcast(I32))
+            src = 8 * c
+            nc.sync.dma_start(planes[c:P:32, :].bitcast(I32), picked_bytes[src:P:32, :].bitcast(I32))
 
-        w_rows = w1.rearrange("(p j) n -> p j n", j=PACK)
-        w_raw = []
-        for hf in range(2):
-            raw = keep.tile([P, PACK, HALF], F32, name=f"w_raw{hf}", tag=f"reuse{hf}", align_bytes=64)
-            nc.sync.dma_start(raw[:], w_rows[:, :, hf * HALF : (hf + 1) * HALF])
-            w_raw.append(raw)
+        w_raw.append(load_w1_half(1, "x_bytes_then_w1"))
 
         d2_words = keep.tile([P, N], U32, name="d2_words", align_bytes=64)
         xq_words = keep.tile([P, S], U32, name="xq_words", align_bytes=64)
         d1_picked = keep.tile([P, H], U32, name="d1_picked", align_bytes=64)
-        nc.vector.tensor_copy(d2_words[:], d_table[:].bitcast(U32).indirect(k2_list[:]))
         nc.vector.tensor_copy(xq_words[:], x_table[:].bitcast(U32).indirect(offs_list[:]))
+        nc.vector.tensor_copy(d2_words[:], d_table[:].bitcast(U32).indirect(k2_list[:]))
         nc.vector.tensor_copy(d1_picked[:], d_table[:].bitcast(U32).indirect(k1_list[:]))
 
         def x_operand(tok):
@@ -88,11 +91,11 @@ def tile_picked_pqskip_relu_p_kernel(
                 **x_operand(tok),
             )
 
-        out_acc = [[], []]
+        first_acc = []
         for m in range(N // P):
             acc = psum.tile([P, HALF], F32, name=f"out_acc0_{m}", tag=f"out_bank{m}")
             shortcut(acc[:], m, slice(0, HALF))
-            out_acc[0].append(acc)
+            first_acc.append(acc)
 
         d1_words = keep.tile([P, H], I32, name="d1_words", align_bytes=64)
         d1_scales = keep.tile([P, H], U8, name="d1_scales", align_bytes=64)
@@ -119,58 +122,81 @@ def tile_picked_pqskip_relu_p_kernel(
                 )
             hidden.append(acc)
 
-        w_codes, w_scales = [], []
+        w_grouped = []
         for hf in range(2):
-            grouped = keep.tile([P, HALF, PACK], BF16, name=f"w_grouped{hf}", align_bytes=64)
+            grouped = keep.tile([P, HALF, PACK], BF16, name=f"w_grouped{hf}", tag=f"rounded{hf}", align_bytes=64)
             nc.scalar.activation(
                 grouped[:].rearrange("p (c i) j -> p c j i", i=4),
                 w_raw[hf][:].rearrange("p j (c i) -> p c j i", i=4),
                 ACT.Copy,
             )
-            codes = keep.tile([P, HALF], U32, name=f"w_codes{hf}", align_bytes=64)
-            scales = keep.tile([P, HALF], U8, name=f"w_scales{hf}", align_bytes=64)
+            w_grouped.append(grouped)
+
+        def quantise(values, name):
+            width = values.shape[1]
+            codes = keep.tile([P, width], U32, name=f"{name}_codes", align_bytes=64)
+            scales = keep.tile([P, width], U8, name=f"{name}_scales", align_bytes=64)
             nc.vector.quantize_mx(
-                out=codes[:].bitcast(FP8X4), scales=scales[:], in_=grouped[:].rearrange("p n j -> p (n j)")
+                out=codes[:].bitcast(FP8X4), scales=scales[:], in_=values.rearrange("p c j -> p (c j)")
             )
-            w_codes.append(codes)
-            w_scales.append(scales)
+            return codes, scales
 
         gain_wide = gain[:].unsqueeze(1).to_broadcast([P, CHUNK, PACK])
-        for hf in range(2):
-            z = keep.tile([P, HALF, PACK], BF16, name=f"z{hf}", align_bytes=64)
-            for c in range(HALF // CHUNK):
-                nc.vector.scalar_tensor_tensor(
-                    out=z[:, c * CHUNK : (c + 1) * CHUNK, :],
-                    in0=hidden[2 * hf + c][:].rearrange("p t s -> p s t"),
-                    scalar=0.0,
-                    in1=gain_wide,
-                    op0=ALU.max,
-                    op1=ALU.mult,
-                )
-            z_codes = keep.tile([P, HALF], U32, name=f"z_codes{hf}", align_bytes=64)
-            z_scales = keep.tile([P, HALF], U8, name=f"z_scales{hf}", align_bytes=64)
-            nc.vector.quantize_mx(
-                out=z_codes[:].bitcast(FP8X4), scales=z_scales[:], in_=z[:].rearrange("p s t -> p (s t)")
+
+        def gated(z, ch):
+            nc.vector.scalar_tensor_tensor(
+                out=z,
+                in0=hidden[ch][:].rearrange("p t s -> p s t"),
+                scalar=0.0,
+                in1=gain_wide,
+                op0=ALU.max,
+                op1=ALU.mult,
             )
-            if hf == 1:
-                for m in range(N // P):
-                    acc = psum.tile([P, HALF], F32, name=f"out_acc1_{m}", tag=f"hidden_bank{m}")
-                    shortcut(acc[:], m, slice(HALF, S))
-                    out_acc[1].append(acc)
-            for m in range(N // P):
-                cols = slice((m % 2) * P, (m % 2 + 1) * P)
-                nc.tensor.matmul_mx(
-                    out=out_acc[hf][m][:],
-                    lhsT=w_codes[m // 2][:, cols].bitcast(FP8X4),
-                    lhsT_scale=w_scales[m // 2][:, cols],
-                    rhs=z_codes[:].bitcast(FP8X4),
-                    rhs_scale=z_scales[:],
-                    start=False,
-                    stop=True,
-                )
-                result = keep.tile([P, HALF], F32, name=f"result{hf}_{m}")
-                if hf == 1 and m % 2 == 1:
-                    nc.vector.tensor_scalar(result[:], out_acc[hf][m][:], 0.0625, None, ALU.mult)
+
+        def dense(acc, m, z_mx):
+            codes, scales = w_mx[m // 2]
+            cols = slice((m % 2) * P, (m % 2 + 1) * P)
+            nc.tensor.matmul_mx(
+                out=acc,
+                lhsT=codes[:, cols].bitcast(FP8X4),
+                lhsT_scale=scales[:, cols],
+                rhs=z_mx[0][:].bitcast(FP8X4),
+                rhs_scale=z_mx[1][:],
+                start=False,
+                stop=True,
+            )
+
+        w_mx = [quantise(w_grouped[0][:], "w0")]
+        z_first = keep.tile([P, HALF, PACK], BF16, name="z_first", tag="rounded0", align_bytes=64)
+        gated(z_first[:, 0:CHUNK, :], 0)
+        gated(z_first[:, CHUNK:HALF, :], 1)
+        w_mx.append(quantise(w_grouped[1][:], "w1"))
+        z_mx = quantise(z_first[:], "z_first")
+        for m in range(N // P):
+            dense(first_acc[m][:], m, z_mx)
+            result = keep.tile([P, HALF], F32, name=f"result_first{m}")
+            nc.scalar.activation(result[:], first_acc[m][:], ACT.Copy, scale=0.0625)
+            nc.sync.dma_start(out[m * P : (m + 1) * P, 0:HALF], result[:])
+
+        z_second = keep.tile([P, HALF, PACK], BF16, name="z_second", tag="rounded1", align_bytes=64)
+        gated(z_second[:, 0:CHUNK, :], 2)
+        gated(z_second[:, CHUNK:HALF, :], 3)
+        out_rows = out.rearrange("(m p) s -> p m s", p=P)
+        for c in range(2):
+            tok = slice(HALF + c * CHUNK, HALF + (c + 1) * CHUNK)
+            accs = [
+                psum.tile([P, 2, CHUNK], F32, name=f"acc{c}_{b}", tag=f"hidden_bank{2 * c + b}") for b in range(2)
+            ]
+            for b in range(2):
+                shortcut(accs[b][:, 0, :], 2 * b, tok)
+            z_mx = quantise(z_second[:, c * CHUNK : (c + 1) * CHUNK, :], f"z_second{c}")
+            for b in range(2):
+                dense(accs[b][:, 0, :], 2 * b, z_mx)
+                shortcut(accs[b][:, 1, :], 2 * b + 1, tok)
+                dense(accs[b][:, 1, :], 2 * b + 1, z_mx)
+                result = keep.tile([P, 2, CHUNK], F32, name=f"result{c}_{b}")
+                if b == 1:
+                    nc.vector.tensor_scalar(result[:], accs[b][:], 0.0625, None, ALU.mult)
                 else:
-                    nc.scalar.activation(result[:], out_acc[hf][m][:], ACT.Copy, scale=0.0625)
-                nc.sync.dma_start(out[m * P : (m + 1) * P, hf * HALF : (hf + 1) * HALF], result[:])
+                    nc.scalar.activation(result[:], accs[b][:], ACT.Copy, scale=0.0625)
+                nc.sync.dma_start(out_rows[:, 2 * b : 2 * b + 2, tok], result[:])

@@ -43,24 +43,16 @@ def tile_picked_pqskip_relu_p_kernel(
         def block_rows(scales):
             return scales[0].bitcast(I32).unsqueeze(1).to_broadcast([16, 8, G // 4])
 
-        w_rows = w1.rearrange("(p j) n -> p j n", j=PACK)
-
-        def load_w1_half(hf, tag):
-            raw = keep.tile([P, PACK, HALF], F32, name=f"w_raw{hf}", tag=tag, align_bytes=64)
-            nc.sync.dma_start(raw[:], w_rows[:, :, hf * HALF : (hf + 1) * HALF])
-            return raw
-
         nc.sync.dma_start(k1_list[:], k1)
-        nc.sync.dma_start(d_bytes[:].bitcast(I32), block_rows(d_scales))
+        nc.scalar.dma_start(d_bytes[:].bitcast(I32), block_rows(d_scales))
         nc.sync.dma_start(k2_list[:], k2)
         nc.sync.dma_start(x_bytes[:].bitcast(I32), block_rows(x_scales))
         nc.sync.dma_start(offs_list[:], offs)
-        nc.sync.dma_start(x_table[:], x_words[0].rearrange("p c r -> p (c r)").bitcast(I32))
         nc.sync.dma_start(d_table[:], d_words[0].rearrange("p c r -> p (c r)").bitcast(I32))
-        w_raw = [load_w1_half(0, "w1_first")]
+        nc.sync.dma_start(x_table[:], x_words[0].rearrange("p c r -> p (c r)").bitcast(I32))
         nc.sync.dma_start(gain[:], gn.rearrange("(p t) o -> p (t o)", t=PACK))
 
-        picked_bytes = keep.tile([P, H + N + S], U8, name="picked_bytes", align_bytes=64)
+        picked_bytes = keep.tile([P, H + N + S], U8, name="picked_bytes", tag="picked_bytes_then_tokens", align_bytes=64)
         k1_cols, k2_cols, x_cols = slice(0, H), slice(H, H + N), slice(H + N, H + N + S)
         nc.vector.tensor_copy(picked_bytes[:, k1_cols], d_bytes[:].indirect(k1_list[:]))
         nc.vector.tensor_copy(picked_bytes[:, k2_cols], d_bytes[:].indirect(k2_list[:]))
@@ -69,33 +61,15 @@ def tile_picked_pqskip_relu_p_kernel(
             src = 8 * c
             nc.sync.dma_start(planes[c:P:32, :].bitcast(I32), picked_bytes[src:P:32, :].bitcast(I32))
 
-        w_raw.append(load_w1_half(1, "x_bytes_then_w1"))
+        w_rows = w1.rearrange("(p j) n -> p j n", j=PACK)
+        w_raw = keep.tile([P, 2, PACK, HALF], F32, name="w_raw", tag="x_bytes_then_w1", align_bytes=64)
+        for hf in range(2):
+            nc.sync.dma_start(w_raw[:, hf], w_rows[:, :, hf * HALF : (hf + 1) * HALF])
 
         d2_words = keep.tile([P, N], U32, name="d2_words", align_bytes=64)
-        xq_words = keep.tile([P, S], U32, name="xq_words", align_bytes=64)
         d1_picked = keep.tile([P, H], U32, name="d1_picked", align_bytes=64)
-        nc.vector.tensor_copy(xq_words[:], x_table[:].bitcast(U32).indirect(offs_list[:]))
-        nc.vector.tensor_copy(d2_words[:], d_table[:].bitcast(U32).indirect(k2_list[:]))
         nc.vector.tensor_copy(d1_picked[:], d_table[:].bitcast(U32).indirect(k1_list[:]))
-
-        def x_operand(tok):
-            return dict(rhs=xq_words[:, tok].bitcast(FP8X4), rhs_scale=planes[:, H + N + tok.start : H + N + tok.stop])
-
-        def shortcut(acc, m, tok):
-            nc.tensor.matmul_mx(
-                out=acc,
-                lhsT=d2_words[:, m * P : (m + 1) * P].bitcast(FP8X4),
-                lhsT_scale=planes[:, H + m * P : H + (m + 1) * P],
-                start=True,
-                stop=False,
-                **x_operand(tok),
-            )
-
-        first_acc = []
-        for m in range(N // P):
-            acc = psum.tile([P, HALF], F32, name=f"out_acc0_{m}", tag=f"out_bank{m}")
-            shortcut(acc[:], m, slice(0, HALF))
-            first_acc.append(acc)
+        nc.vector.tensor_copy(d2_words[:], d_table[:].bitcast(U32).indirect(k2_list[:]))
 
         d1_words = keep.tile([P, H], I32, name="d1_words", align_bytes=64)
         d1_scales = keep.tile([P, H], U8, name="d1_scales", align_bytes=64)
@@ -108,8 +82,27 @@ def tile_picked_pqskip_relu_p_kernel(
             planes[:, k1_cols].rearrange("p (m t) -> p m t", t=PACK),
         )
 
-        hidden = []
-        for ch in range(S // CHUNK):
+        xq_words = keep.tile([P, S], U32, name="xq_words", tag="picked_bytes_then_tokens", align_bytes=64)
+        for hf in range(2):
+            entries = offs_list[:, hf * HALF // 16 : (hf + 1) * HALF // 16]
+            nc.vector.tensor_copy(xq_words[:, hf * HALF : (hf + 1) * HALF], x_table[:].bitcast(U32).indirect(entries))
+
+        def x_operand(tok):
+            return dict(
+                rhs=xq_words[:, tok].bitcast(FP8X4), rhs_scale=planes[:, H + N + tok.start : H + N + tok.stop]
+            )
+
+        def shortcut(acc, m, tok):
+            nc.tensor.matmul_mx(
+                out=acc,
+                lhsT=d2_words[:, m * P : (m + 1) * P].bitcast(FP8X4),
+                lhsT_scale=planes[:, H + m * P : H + (m + 1) * P],
+                start=True,
+                stop=False,
+                **x_operand(tok),
+            )
+
+        def hidden_chunk(ch):
             acc = psum.tile([P, PACK, CHUNK], F32, name=f"hidden{ch}", tag=f"hidden_bank{ch}")
             for t in range(PACK):
                 nc.tensor.matmul_mx(
@@ -120,14 +113,22 @@ def tile_picked_pqskip_relu_p_kernel(
                     stop=True,
                     **x_operand(slice(ch * CHUNK, (ch + 1) * CHUNK)),
                 )
-            hidden.append(acc)
+            return acc
+
+        hidden = [hidden_chunk(0), hidden_chunk(1)]
+        first_acc = []
+        for m in range(N // P):
+            acc = psum.tile([P, HALF], F32, name=f"out_acc0_{m}", tag=f"out_bank{m}")
+            shortcut(acc[:], m, slice(0, HALF))
+            first_acc.append(acc)
+        hidden.extend([hidden_chunk(2), hidden_chunk(3)])
 
         w_grouped = []
         for hf in range(2):
             grouped = keep.tile([P, HALF, PACK], BF16, name=f"w_grouped{hf}", tag=f"rounded{hf}", align_bytes=64)
             nc.scalar.activation(
                 grouped[:].rearrange("p (c i) j -> p c j i", i=4),
-                w_raw[hf][:].rearrange("p j (c i) -> p c j i", i=4),
+                w_raw[:, hf].rearrange("p j (c i) -> p c j i", i=4),
                 ACT.Copy,
             )
             w_grouped.append(grouped)
@@ -195,8 +196,9 @@ def tile_picked_pqskip_relu_p_kernel(
                 shortcut(accs[b][:, 1, :], 2 * b + 1, tok)
                 dense(accs[b][:, 1, :], 2 * b + 1, z_mx)
                 result = keep.tile([P, 2, CHUNK], F32, name=f"result{c}_{b}")
-                if b == 1:
+                if c == 1 and b == 1:
                     nc.vector.tensor_scalar(result[:], accs[b][:], 0.0625, None, ALU.mult)
                 else:
                     nc.scalar.activation(result[:], accs[b][:], ACT.Copy, scale=0.0625)
-                nc.sync.dma_start(out_rows[:, 2 * b : 2 * b + 2, tok], result[:])
+                queue = nc.scalar if c == 1 and b == 0 else nc.sync
+                queue.dma_start(out_rows[:, 2 * b : 2 * b + 2, tok], result[:])

@@ -74,12 +74,12 @@ def tile_picked_pqskip_relu_p_kernel(
         d1_words = keep.tile([P, H], I32, name="d1_words", align_bytes=64)
         d1_scales = keep.tile([P, H], U8, name="d1_scales", align_bytes=64)
         nc.vector.tensor_copy(
-            d1_words[:].rearrange("p (t m) -> p m t", t=PACK),
-            d1_picked[:].bitcast(I32).rearrange("p (m t) -> p m t", t=PACK),
+            d1_words[:].rearrange("p (t b i) -> p b t i", t=PACK, i=4),
+            d1_picked[:].bitcast(I32).rearrange("p (b i t) -> p b t i", t=PACK, i=4),
         )
         nc.vector.tensor_copy(
-            d1_scales[:].rearrange("p (t m) -> p m t", t=PACK),
-            planes[:, k1_cols].rearrange("p (m t) -> p m t", t=PACK),
+            d1_scales[:].rearrange("p (t m) -> p t m", t=PACK),
+            planes[:, k1_cols].rearrange("p (m t) -> p t m", t=PACK),
         )
 
         xq_words = keep.tile([P, S], U32, name="xq_words", tag="picked_bytes_then_tokens", align_bytes=64)

@@ -43,8 +43,8 @@ def tile_picked_pqskip_relu_p_kernel(
         def block_rows(scales):
             return scales[0].bitcast(I32).unsqueeze(1).to_broadcast([16, 8, G // 4])
 
+        nc.sync.dma_start(d_bytes[:].bitcast(I32), block_rows(d_scales))
         nc.sync.dma_start(k1_list[:], k1)
-        nc.scalar.dma_start(d_bytes[:].bitcast(I32), block_rows(d_scales))
         nc.sync.dma_start(k2_list[:], k2)
         nc.sync.dma_start(x_bytes[:].bitcast(I32), block_rows(x_scales))
         nc.sync.dma_start(offs_list[:], offs)
@@ -133,9 +133,9 @@ def tile_picked_pqskip_relu_p_kernel(
             )
             w_grouped.append(grouped)
 
-        def quantise(values, name):
+        def quantise(values, name, codes_tag=None):
             width = values.shape[1]
-            codes = keep.tile([P, width], U32, name=f"{name}_codes", align_bytes=64)
+            codes = keep.tile([P, width], U32, name=f"{name}_codes", tag=codes_tag or f"{name}_codes", align_bytes=64)
             scales = keep.tile([P, width], U8, name=f"{name}_scales", align_bytes=64)
             nc.vector.quantize_mx(
                 out=codes[:].bitcast(FP8X4), scales=scales[:], in_=values.rearrange("p c j -> p (c j)")
@@ -167,12 +167,12 @@ def tile_picked_pqskip_relu_p_kernel(
                 stop=True,
             )
 
-        w_mx = [quantise(w_grouped[0][:], "w0")]
-        z_first = keep.tile([P, HALF, PACK], BF16, name="z_first", tag="rounded0", align_bytes=64)
+        z_first = keep.tile([P, HALF, PACK], BF16, name="z_first", align_bytes=64)
         gated(z_first[:, 0:CHUNK, :], 0)
         gated(z_first[:, CHUNK:HALF, :], 1)
+        w_mx = [quantise(w_grouped[0][:], "w0")]
+        z_mx = quantise(z_first[:], "z_first", "rounded0")
         w_mx.append(quantise(w_grouped[1][:], "w1"))
-        z_mx = quantise(z_first[:], "z_first")
         for m in range(N // P):
             dense(first_acc[m][:], m, z_mx)
             result = keep.tile([P, HALF], F32, name=f"result_first{m}")

from contextlib import ExitStack

import concourse.mybir as mybir

F32 = mybir.dt.float32
BF16 = mybir.dt.bfloat16
I32 = mybir.dt.int32
U32 = mybir.dt.uint32
U16 = mybir.dt.uint16
U8 = mybir.dt.uint8
FP8X4 = mybir.dt.float8_e4m3fn_x4
ALU = mybir.AluOpType
ACT = mybir.ActivationFunctionType

P = 128
PACK = 4
K, T, S, N, G, H = 512, 2048, 512, 512, 2048, 512
CHUNK = 128
HALF = 256
FLOPS = 2 * K * H * S + 2 * K * N * S + 2 * H * N * S


def tile_picked_pqskip_relu_p_kernel(
    tc, x_words, x_scales, d_words, d_scales, gn, w1, offs, k1, k2, out
):
    nc = tc.nc
    with ExitStack() as ctx:
        keep = ctx.enter_context(tc.tile_pool(name="keep", bufs=1))
        psum = ctx.enter_context(tc.psum_pool(name="psum", bufs=1))

        k1_list = keep.tile([P, H // 16], U16, name="k1_list")
        k2_list = keep.tile([P, N // 16], U16, name="k2_list")
        offs_list = keep.tile([P, S // 16], U16, name="offs_list")
        d_bytes = keep.tile([P, G], U8, name="d_bytes", align_bytes=64)
        x_bytes = keep.tile([P, T], U8, name="x_bytes", tag="x_bytes_then_w1", align_bytes=64)
        d_table = keep.tile([P, G], I32, name="d_table", align_bytes=64)
        x_table = keep.tile([P, T], I32, name="x_table", align_bytes=64)
        gain = keep.tile([P, PACK], F32, name="gain")
        planes = keep.tile([P, H + N + S], U8, name="planes", align_bytes=64)

        nc.vector.memset(planes[:].bitcast(I32), 0)

        def block_rows(scales):
            return scales[0].bitcast(I32).unsqueeze(1).to_broadcast([16, 8, G // 4])

        nc.sync.dma_start(d_bytes[:].bitcast(I32), block_rows(d_scales))
        nc.sync.dma_start(k1_list[:], k1)
        nc.sync.dma_start(k2_list[:], k2)
        nc.sync.dma_start(x_bytes[:].bitcast(I32), block_rows(x_scales))
        nc.sync.dma_start(offs_list[:], offs)
        nc.sync.dma_start(d_table[:], d_words[0].rearrange("p c r -> p (c r)").bitcast(I32))
        nc.sync.dma_start(x_table[:], x_words[0].rearrange("p c r -> p (c r)").bitcast(I32))
        nc.sync.dma_start(gain[:], gn.rearrange("(p t) o -> p (t o)", t=PACK))

        picked_bytes = keep.tile([P, H + N + S], U8, name="picked_bytes", tag="picked_bytes_then_tokens", align_bytes=64)
        k1_cols, k2_cols, x_cols = slice(0, H), slice(H, H + N), slice(H + N, H + N + S)
        nc.vector.tensor_copy(picked_bytes[:, k1_cols], d_bytes[:].indirect(k1_list[:]))
        nc.vector.tensor_copy(picked_bytes[:, k2_cols], d_bytes[:].indirect(k2_list[:]))
        nc.vector.tensor_copy(picked_bytes[:, x_cols], x_bytes[:].indirect(offs_list[:]))
        for c in range(4):
            src = 8 * c
            nc.sync.dma_start(planes[c:P:32, :].bitcast(I32), picked_bytes[src:P:32, :].bitcast(I32))

        w_rows = w1.rearrange("(p j) n -> p j n", j=PACK)
        w_raw = keep.tile([P, 2, PACK, HALF], F32, name="w_raw", tag="x_bytes_then_w1", align_bytes=64)
        for hf in range(2):
            nc.sync.dma_start(w_raw[:, hf], w_rows[:, :, hf * HALF : (hf + 1) * HALF])

        d2_words = keep.tile([P, N], U32, name="d2_words", align_bytes=64)
        d1_picked = keep.tile([P, H], U32, name="d1_picked", align_bytes=64)
        nc.vector.tensor_copy(d1_picked[:], d_table[:].bitcast(U32).indirect(k1_list[:]))
        nc.vector.tensor_copy(d2_words[:], d_table[:].bitcast(U32).indirect(k2_list[:]))

        d1_words = keep.tile([P, H], I32, name="d1_words", align_bytes=64)
        d1_scales = keep.tile([P, H], U8, name="d1_scales", align_bytes=64)
        nc.vector.tensor_copy(
            d1_words[:].rearrange("p (t b i) -> p b t i", t=PACK, i=4),
            d1_picked[:].bitcast(I32).rearrange("p (b i t) -> p b t i", t=PACK, i=4),
        )
        nc.vector.tensor_copy(
            d1_scales[:].rearrange("p (t m) -> p t m", t=PACK),
            planes[:, k1_cols].rearrange("p (m t) -> p t m", t=PACK),
        )

        xq_words = keep.tile([P, S], U32, name="xq_words", tag="picked_bytes_then_tokens", align_bytes=64)
        for hf in range(2):
            entries = offs_list[:, hf * HALF // 16 : (hf + 1) * HALF // 16]
            nc.vector.tensor_copy(xq_words[:, hf * HALF : (hf + 1) * HALF], x_table[:].bitcast(U32).indirect(entries))

        def x_operand(tok):
            return dict(
                rhs=xq_words[:, tok].bitcast(FP8X4), rhs_scale=planes[:, H + N + tok.start : H + N + tok.stop]
            )

        def shortcut(acc, m, tok):
            nc.tensor.matmul_mx(
                out=acc,
                lhsT=d2_words[:, m * P : (m + 1) * P].bitcast(FP8X4),
                lhsT_scale=planes[:, H + m * P : H + (m + 1) * P],
                start=True,
                stop=False,
                **x_operand(tok),
            )

        def hidden_chunk(ch):
            acc = psum.tile([P, PACK, CHUNK], F32, name=f"hidden{ch}", tag=f"hidden_bank{ch}")
            for t in range(PACK):
                nc.tensor.matmul_mx(
                    out=acc[:, t, :],
                    lhsT=d1_words[:, t * P : (t + 1) * P].bitcast(FP8X4),
                    lhsT_scale=d1_scales[:, t * P : (t + 1) * P],
                    start=True,
                    stop=True,
                    **x_operand(slice(ch * CHUNK, (ch + 1) * CHUNK)),
                )
            return acc

        hidden = [hidden_chunk(0), hidden_chunk(1)]
        first_acc = []
        for m in range(N // P):
            acc = psum.tile([P, HALF], F32, name=f"out_acc0_{m}", tag=f"out_bank{m}")
            shortcut(acc[:], m, slice(0, HALF))
            first_acc.append(acc)
        hidden.extend([hidden_chunk(2), hidden_chunk(3)])

        w_grouped = []
        for hf in range(2):
            grouped = keep.tile([P, HALF, PACK], BF16, name=f"w_grouped{hf}", tag=f"rounded{hf}", align_bytes=64)
            nc.scalar.activation(
                grouped[:].rearrange("p (c i) j -> p c j i", i=4),
                w_raw[:, hf].rearrange("p j (c i) -> p c j i", i=4),
                ACT.Copy,
            )
            w_grouped.append(grouped)

        def quantise(values, name, codes_tag=None):
            width = values.shape[1]
            codes = keep.tile([P, width], U32, name=f"{name}_codes", tag=codes_tag or f"{name}_codes", align_bytes=64)
            scales = keep.tile([P, width], U8, name=f"{name}_scales", align_bytes=64)
            nc.vector.quantize_mx(
                out=codes[:].bitcast(FP8X4), scales=scales[:], in_=values.rearrange("p c j -> p (c j)")
            )
            return codes, scales

        gain_wide = gain[:].unsqueeze(1).to_broadcast([P, CHUNK, PACK])

        def gated(z, ch):
            nc.vector.scalar_tensor_tensor(
                out=z,
                in0=hidden[ch][:].rearrange("p t s -> p s t"),
                scalar=0.0,
                in1=gain_wide,
                op0=ALU.max,
                op1=ALU.mult,
            )

        def dense(acc, m, z_mx):
            codes, scales = w_mx[m // 2]
            cols = slice((m % 2) * P, (m % 2 + 1) * P)
            nc.tensor.matmul_mx(
                out=acc,
                lhsT=codes[:, cols].bitcast(FP8X4),
                lhsT_scale=scales[:, cols],
                rhs=z_mx[0][:].bitcast(FP8X4),
                rhs_scale=z_mx[1][:],
                start=False,
                stop=True,
            )

        z_first = keep.tile([P, HALF, PACK], BF16, name="z_first", align_bytes=64)
        gated(z_first[:, 0:CHUNK, :], 0)
        gated(z_first[:, CHUNK:HALF, :], 1)
        w_mx = [quantise(w_grouped[0][:], "w0")]
        z_mx = quantise(z_first[:], "z_first", "rounded0")
        w_mx.append(quantise(w_grouped[1][:], "w1"))
        for m in range(N // P):
            dense(first_acc[m][:], m, z_mx)
            result = keep.tile([P, HALF], F32, name=f"result_first{m}")
            nc.scalar.activation(result[:], first_acc[m][:], ACT.Copy, scale=0.0625)
            nc.sync.dma_start(out[m * P : (m + 1) * P, 0:HALF], result[:])

        z_second = keep.tile([P, HALF, PACK], BF16, name="z_second", tag="rounded1", align_bytes=64)
        gated(z_second[:, 0:CHUNK, :], 2)
        gated(z_second[:, CHUNK:HALF, :], 3)
        out_rows = out.rearrange("(m p) s -> p m s", p=P)
        for c in range(2):
            tok = slice(HALF + c * CHUNK, HALF + (c + 1) * CHUNK)
            accs = [
                psum.tile([P, 2, CHUNK], F32, name=f"acc{c}_{b}", tag=f"hidden_bank{2 * c + b}") for b in range(2)
            ]
            for b in range(2):
                shortcut(accs[b][:, 0, :], 2 * b, tok)
            z_mx = quantise(z_second[:, c * CHUNK : (c + 1) * CHUNK, :], f"z_second{c}")
            for b in range(2):
                dense(accs[b][:, 0, :], 2 * b, z_mx)
                shortcut(accs[b][:, 1, :], 2 * b + 1, tok)
                dense(accs[b][:, 1, :], 2 * b + 1, z_mx)
                result = keep.tile([P, 2, CHUNK], F32, name=f"result{c}_{b}")
                if c == 1 and b == 1:
                    nc.vector.tensor_scalar(result[:], accs[b][:], 0.0625, None, ALU.mult)
                else:
                    nc.scalar.activation(result[:], accs[b][:], ACT.Copy, scale=0.0625)
                queue = nc.scalar if c == 1 and b == 0 else nc.sync
                queue.dma_start(out_rows[:, 2 * b : 2 * b + 2, tok], result[:])
